import numpy as np
import ml_dtypes


def mxq(x, axis, fmt="e4m3"):
    dtype, down = {"e4m3": (ml_dtypes.float8_e4m3fn, 7), "e5m2": (ml_dtypes.float8_e5m2, 14)}[fmt]
    v = np.moveaxis(np.asarray(x, np.float32).astype(ml_dtypes.bfloat16).astype(np.float64), axis, -1)
    blocks = v.reshape(v.shape[:-1] + (-1, 32))
    amax = np.abs(blocks).max(-1, keepdims=True)
    byte = np.maximum(np.where(amax > 0, np.frexp(amax)[1] - 1 + 127, 0) - down, 1)
    scale = np.exp2(byte - 127.0)
    codes = (blocks / scale).astype(np.float32).astype(dtype).astype(np.float64)
    return np.moveaxis((codes * scale).reshape(v.shape), -1, axis)


WIDE = False


def mx_kscale(k):
    if not WIDE:
        return np.ones(k)
    levels = np.array([10, -10, 5, -5, 0])
    if k % 512:
        return np.exp2(np.random.permutation(np.resize(levels, k // 32))).repeat(32)
    a = np.empty((k // 512, 16))
    for p in range(k // 512):
        a[p, :8] = np.random.permutation(np.resize(levels, 8))
        for g in range(8):
            far = levels[np.abs(levels - a[p, g]) >= 10]
            a[p, g + 8] = far[np.random.randint(len(far))]
    return np.exp2(a.ravel()).repeat(32)


def f64(x):
    return np.asarray(x).astype(np.float64)


def striped(idx):
    return np.tile(idx.reshape(-1, 16).T, (8, 1)).astype(np.uint16)


def unstriped(offs):
    return offs[:16].T.reshape(-1).astype(np.int64)


def pack_weight(w):
    k, n = w.shape
    w = f64(np.asarray(w, np.float32).astype(ml_dtypes.bfloat16)).reshape(k // 32, 32, n)
    amax = np.abs(w).max(1)
    byte = np.clip(np.where(amax > 0, np.frexp(amax)[1] - 1 + 127 - 7, 1), 1, 254)
    scaled = (w * np.exp2(127.0 - byte)[:, None, :]).reshape(k, n).astype(np.float32)
    words = np.ascontiguousarray(scaled.reshape(k // 512, 128, 4, n).transpose(0, 1, 3, 2)).astype(ml_dtypes.float8_e4m3fn).view(np.uint8)
    return words, np.ascontiguousarray(byte.astype(np.uint8).reshape(k // 512, 16, n))


def unpack_weight(words, scales):
    g, p, n, _ = words.shape
    vals = np.ascontiguousarray(words).view(ml_dtypes.float8_e4m3fn).astype(np.float64) * np.repeat(np.exp2(scales.astype(np.float64) - 127.0), 8, axis=1)[..., None]
    return vals.transpose(0, 1, 3, 2).reshape(g * 512, n)


def relu(v):
    return np.maximum(v, 0.0)


def gelu(v):
    return 0.5 * v * (1.0 + np.tanh(np.sqrt(2.0 / np.pi) * (v + 0.044715 * v**3)))


K, T, S, D, V, H, N, U = 512, 4096, 1024, 2, 512, 512, 128, 256
P = 2 ** 7


def setup_inputs():
    n = np.random.standard_normal
    s = mx_kscale(K)[:, None]
    u = mx_kscale(H)
    packed_xT = pack_weight(n((K, T)) * s)
    return {
        "x_words": packed_xT[0],
        "x_scales": packed_xT[1],
        "w1": (n((K, H)) / np.sqrt(K) / s * u).astype(np.float32),
        "w2": (n((H, N)) / np.sqrt(H) / u[:, None]).astype(np.float32),
        "gate": (np.tile(np.random.uniform(0.2, 1.0, (D, 1, V)) / np.sqrt(D), (1, P, 1))).astype(np.float32),
        "gate2": (np.tile(np.random.uniform(0.2, 1.0, (D, 1, U)) / np.sqrt(D), (1, P, 1))).astype(np.float32),
        "offs": striped(np.random.permutation(T)[:S]),
        "pos1": striped(np.random.permutation(S)[:V]),
        "pos2": striped(np.random.permutation(S)[:V]),
        "nxt1": striped(np.random.permutation(V)[:U]),
        "nxt2": striped(np.random.permutation(V)[:U]),
    }


def reference(x_words, x_scales, w1, w2, gate, gate2, offs, pos1, pos2, nxt1, nxt2):
    xq = unpack_weight(x_words, x_scales)[:, unstriped(offs)]
    h = gelu(mxq(f64(w1), 0, "e4m3").T @ xq)
    z = h[:, unstriped(pos1)] * f64(gate)[0, :1] + h[:, unstriped(pos2)] * f64(gate)[1, :1]
    g = relu(mxq(f64(w2), 0, "e4m3").T @ mxq(z, 0, "e4m3"))
    return g[:, unstriped(nxt1)] * f64(gate2)[0, :1] + g[:, unstriped(nxt2)] * f64(gate2)[1, :1]

@@ -1,0 +1,189 @@
+from contextlib import ExitStack
+
+import concourse.mybir as mybir
+from concourse.masks import make_identity
+
+K, T, S, V, H, N, U = 512, 4096, 1024, 512, 512, 128, 256
+FLOPS = 2 * K * H * S + 2 * H * N * V
+
+F32 = mybir.dt.float32
+BF16 = mybir.dt.bfloat16
+I32 = mybir.dt.int32
+U32 = mybir.dt.uint32
+U16 = mybir.dt.uint16
+U8 = mybir.dt.uint8
+FP8X4 = mybir.dt.float8_e4m3fn_x4
+MULT = mybir.AluOpType.mult
+ADD = mybir.AluOpType.add
+GELU = mybir.ActivationFunctionType.Gelu_apprx_tanh
+RELU = mybir.ActivationFunctionType.Relu
+
+P = 128
+PACK = 4
+BANK = 512
+TILES = H // P
+GROUPS = ((0, 256), (256, 384), (384, 512))
+WORDS_FIRST = 1024
+
+
+def tile_picked_hop2_gelu_p_kernel(tc, x_words, x_scales, w1, w2, gate, gate2, offs, pos1, pos2, nxt1, nxt2, out):
+    nc = tc.nc
+    with ExitStack() as ctx:
+        keep = ctx.enter_context(tc.tile_pool(name="keep", bufs=1))
+        psum = ctx.enter_context(tc.psum_pool(name="psum", bufs=2))
+
+        def load_list(name, src):
+            tile = keep.tile(list(src.shape), U16, name=name)
+            nc.sync.dma_start(tile[:], src)
+            return tile
+
+        ident = keep.tile([P, P], F32, name="ident")
+        make_identity(nc, ident[:])
+
+        warm_in = keep.tile([P, 1], F32, name="warm_in")
+        warm_out = keep.tile([P, 1], F32, name="warm_out")
+        nc.gpsimd.memset(warm_in[:], 0.0)
+        nc.scalar.activation(warm_out[:], warm_in[:], GELU)
+
+        scale_table = keep.tile([P, T], U8, name="scale_table")
+        nc.vector.memset(scale_table[:].bitcast(I32), 0)
+
+        word_table = keep.tile([P, T], U32, name="word_table")
+        words_hbm = x_words[0].rearrange("p n t -> p (n t)").bitcast(I32)
+        offs_sb = load_list("offs_sb", offs)
+        nc.sync.dma_start(word_table[:, :WORDS_FIRST].bitcast(I32), words_hbm[:, :WORDS_FIRST])
+        for q in range(4):
+            nc.sync.dma_start(scale_table[32 * q : 32 * q + 4, :].bitcast(I32), x_scales[0, 4 * q : 4 * q + 4, :].bitcast(I32))
+        nc.sync.dma_start(word_table[:, WORDS_FIRST:].bitcast(I32), words_hbm[:, WORDS_FIRST:])
+
+        w1_hbm = w1.rearrange("(p j) c -> p j c", j=PACK)
+        w1_raw = [keep.tile([P, PACK, P], F32, name=f"w1_raw{t}") for t in range(TILES)]
+        gates = [keep.tile([P, V], F32, name=f"gate{d}") for d in range(2)]
+        for t in range(3):
+            nc.sync.dma_start(w1_raw[t][:], w1_hbm[:, :, t * P : (t + 1) * P])
+        pos = [load_list("pos1_sb", pos1), load_list("pos2_sb", pos2)]
+        nc.sync.dma_start(gates[0][:], gate[0])
+        nc.sync.dma_start(w1_raw[3][:], w1_hbm[:, :, 3 * P :])
+        nc.sync.dma_start(gates[1][:], gate[1])
+        w2_raw = keep.tile([P, PACK, N], F32, name="w2_raw")
+        nc.sync.dma_start(w2_raw[:], w2.rearrange("(p j) c -> p j c", j=PACK))
+        nxt = [load_list("nxt1_sb", nxt1), load_list("nxt2_sb", nxt2)]
+        gates2 = keep.tile([P, 2, U], F32, name="gates2")
+        nc.sync.dma_start(gates2[:], gate2.rearrange("d p r -> p d r"))
+
+        def quantise(name, values, width):
+            codes = keep.tile([P, width], U32, name=name + "_codes", align_bytes=64)
+            scales = keep.tile([P, width], U8, name=name + "_scales", align_bytes=64)
+            nc.vector.quantize_mx(out=codes[:].bitcast(FP8X4), scales=scales[:], in_=values)
+            return codes, scales
+
+        def quantise_weight(name, raw, copy):
+            grouped = keep.tile([P, P * PACK], BF16, name=name + "_grouped", tag=name + "_grouped", align_bytes=64)
+            copy(
+                grouped[:].rearrange("p (c i j) -> p c j i", i=4, j=PACK),
+                raw[:].rearrange("p j (c i) -> p c j i", i=4),
+            )
+            return quantise(name, grouped[:], P)
+
+        def product(acc, stationary, moving):
+            nc.tensor.matmul_mx(
+                out=acc,
+                lhsT=stationary[0][:].bitcast(FP8X4),
+                lhsT_scale=stationary[1][:],
+                rhs=moving[0].bitcast(FP8X4),
+                rhs_scale=moving[1],
+                start=True,
+                stop=True,
+            )
+
+        x_bytes = keep.tile([P, S], U8, name="x_bytes", align_bytes=64)
+        nc.vector.tensor_copy(x_bytes[:], scale_table[:].indirect(offs_sb[:]))
+        halves = S // BANK
+
+        def pick_words(c, tag):
+            codes = keep.tile([P, BANK], U32, name=f"x_codes{c}", tag=tag, align_bytes=64)
+            nc.vector.tensor_copy(codes[:], word_table[:].indirect(offs_sb[:, c * BANK // 16 : (c + 1) * BANK // 16]))
+            return codes
+
+        x_codes = [pick_words(0, "x_codes0")]
+        w1_q = [quantise_weight("w1_0", w1_raw[0], nc.scalar.copy)]
+        x_codes.append(pick_words(1, "w1_0_grouped"))
+        w1_q.append(quantise_weight("w1_1", w1_raw[1], nc.scalar.copy))
+        for t in range(2, TILES):
+            w1_q.append(quantise_weight(f"w1_{t}", w1_raw[t], nc.vector.tensor_copy))
+
+        h = [keep.tile([P, S], F32, name=f"h{t}") for t in range(TILES)]
+
+        def hidden(t):
+            weights = w1_q[t]
+            for c in range(halves):
+                cols = slice(c * BANK, (c + 1) * BANK)
+                acc = psum.tile([P, BANK], F32, name="h_acc")
+                product(acc[:], weights, (x_codes[c][:], x_bytes[:, cols]))
+                nc.scalar.activation(h[t][:, cols], acc[:], GELU)
+
+        z_rows = [keep.tile([P, (v1 - v0) // P, 2, P, 2], BF16, name=f"z_rows{v0}") for v0, v1 in GROUPS]
+
+        def aggregate(t, first, last):
+            v0, v1 = GROUPS[first][0], GROUPS[last][1]
+            terms = []
+            for d in range(2):
+                term = keep.tile([P, v1 - v0], F32, name=f"term{d}_{t}_{v0}")
+                nc.vector.tensor_tensor(term[:], h[t][:].indirect(pos[d][:, v0 // 16 : v1 // 16]), gates[d][:, v0:v1], MULT)
+                terms.append(term)
+            turned = psum.tile([P, v1 - v0], F32, name="turned", tag="turned")
+            for b in range((v1 - v0) // P):
+                cols = slice(b * P, (b + 1) * P)
+                for d in range(2):
+                    nc.tensor.matmul(turned[:, cols], terms[d][:, cols], ident[:], start=(d == 0), stop=(d == 1), is_transpose=True)
+            for g in range(first, last + 1):
+                g0, g1 = GROUPS[g]
+                nc.scalar.copy(
+                    z_rows[g][:, :, :, 32 * t : 32 * (t + 1), :],
+                    turned[:, g0 - v0 : g1 - v0].rearrange("v (b p u e) -> v b u p e", p=32, u=2, e=2),
+                )
+
+        g_all = keep.tile([P, V], F32, name="g_all")
+
+        def requantise(g):
+            v0, v1 = GROUPS[g]
+            blocks = (v1 - v0) // P
+            words = z_rows[g][:].rearrange("v b u p e -> v (b u p e)").bitcast(F32)
+            back = psum.tile([P, blocks, 2, P], F32, name="back")
+            for b in range(blocks):
+                for u in range(2):
+                    nc.tensor.transpose(back[:, b, u, :], words[:, (2 * b + u) * P : (2 * b + u + 1) * P], ident[:])
+            z_grouped = keep.tile([P, (v1 - v0) * PACK], BF16, name=f"z_grouped{g}", align_bytes=64)
+            nc.scalar.copy(
+                z_grouped[:].bitcast(F32).rearrange("p (b v u) -> p b v u", b=blocks, u=2),
+                back[:].rearrange("p b u v -> p b v u"),
+            )
+            return quantise(f"z{g}", z_grouped[:], v1 - v0)
+
+        def second_layer(g, z_q, tag):
+            v0, v1 = GROUPS[g]
+            acc = psum.tile([P, v1 - v0], F32, name="g_acc", tag=tag)
+            product(acc[:], w2_q, (z_q[0][:], z_q[1][:]))
+            nc.scalar.activation(g_all[:, v0:v1], acc[:], RELU)
+
+        for t in range(TILES):
+            hidden(t)
+        w2_q = quantise_weight("w2", w2_raw, nc.scalar.copy)
+        aggregate(0, 0, 2)
+        aggregate(1, 0, 2)
+        z_q = []
+        for g in range(len(GROUPS)):
+            aggregate(2, g, g)
+            if g > 0:
+                z_q.append(requantise(g - 1))
+            aggregate(3, g, g)
+        z_q.append(requantise(len(GROUPS) - 1))
+        for g in range(len(GROUPS)):
+            second_layer(g, z_q[g], "turned" if g < len(GROUPS) - 1 else "g_acc")
+
+        roots = [keep.tile([P, U], F32, name=f"root{d}") for d in range(2)]
+        for d in range(2):
+            nc.vector.tensor_tensor(roots[d][:], g_all[:].indirect(nxt[d][:]), gates2[:, d, :], MULT)
+        result = keep.tile([P, U], F32, name="result")
+        nc.vector.tensor_tensor(result[:], roots[0][:], roots[1][:], ADD)
+        nc.sync.dma_start(out, result[:])

@@ -40,11 +40,6 @@ def tile_picked_hop2_gelu_p_kernel(tc, x_words, x_scales, w1, w2, gate, gate2, o
         ident = keep.tile([P, P], F32, name="ident")
         make_identity(nc, ident[:])
 
-        warm_in = keep.tile([P, 1], F32, name="warm_in")
-        warm_out = keep.tile([P, 1], F32, name="warm_out")
-        nc.gpsimd.memset(warm_in[:], 0.0)
-        nc.scalar.activation(warm_out[:], warm_in[:], GELU)
-
         scale_table = keep.tile([P, T], U8, name="scale_table")
         nc.vector.memset(scale_table[:].bitcast(I32), 0)
 
@@ -52,44 +47,45 @@ def tile_picked_hop2_gelu_p_kernel(tc, x_words, x_scales, w1, w2, gate, gate2, o
         words_hbm = x_words[0].rearrange("p n t -> p (n t)").bitcast(I32)
         offs_sb = load_list("offs_sb", offs)
         nc.sync.dma_start(word_table[:, :WORDS_FIRST].bitcast(I32), words_hbm[:, :WORDS_FIRST])
-        for q in range(4):
-            nc.sync.dma_start(scale_table[32 * q : 32 * q + 4, :].bitcast(I32), x_scales[0, 4 * q : 4 * q + 4, :].bitcast(I32))
+        for r in range(4):
+            nc.sync.dma_start(scale_table[r:P:32, :].bitcast(I32), x_scales[0, r:16:4, :].bitcast(I32))
         nc.sync.dma_start(word_table[:, WORDS_FIRST:].bitcast(I32), words_hbm[:, WORDS_FIRST:])
 
         w1_hbm = w1.rearrange("(p j) c -> p j c", j=PACK)
-        w1_raw = [keep.tile([P, PACK, P], F32, name=f"w1_raw{t}") for t in range(TILES)]
+        w1_early = [keep.tile([P, PACK, P], F32, name=f"w1_raw{t}") for t in range(2)]
+        w1_late = keep.tile([P, PACK, 2 * P], F32, name="w1_late")
         gates = [keep.tile([P, V], F32, name=f"gate{d}") for d in range(2)]
-        for t in range(3):
-            nc.sync.dma_start(w1_raw[t][:], w1_hbm[:, :, t * P : (t + 1) * P])
+        for t in range(2):
+            nc.sync.dma_start(w1_early[t][:], w1_hbm[:, :, t * P : (t + 1) * P])
+        nc.sync.dma_start(w1_late[:], w1_hbm[:, :, 2 * P :])
         pos = [load_list("pos1_sb", pos1), load_list("pos2_sb", pos2)]
-        nc.sync.dma_start(gates[0][:], gate[0])
-        nc.sync.dma_start(w1_raw[3][:], w1_hbm[:, :, 3 * P :])
-        nc.sync.dma_start(gates[1][:], gate[1])
+        for d in range(2):
+            nc.sync.dma_start(gates[d][:], gate[d])
         w2_raw = keep.tile([P, PACK, N], F32, name="w2_raw")
         nc.sync.dma_start(w2_raw[:], w2.rearrange("(p j) c -> p j c", j=PACK))
         nxt = [load_list("nxt1_sb", nxt1), load_list("nxt2_sb", nxt2)]
         gates2 = keep.tile([P, 2, U], F32, name="gates2")
         nc.sync.dma_start(gates2[:], gate2.rearrange("d p r -> p d r"))
 
-        def quantise(name, values, width):
-            codes = keep.tile([P, width], U32, name=name + "_codes", align_bytes=64)
+        def quantise(name, values, width, codes_tag=""):
+            codes = keep.tile([P, width], U32, name=name + "_codes", tag=codes_tag or name + "_codes", align_bytes=64)
             scales = keep.tile([P, width], U8, name=name + "_scales", align_bytes=64)
             nc.vector.quantize_mx(out=codes[:].bitcast(FP8X4), scales=scales[:], in_=values)
             return codes, scales
 
-        def quantise_weight(name, raw, copy):
-            grouped = keep.tile([P, P * PACK], BF16, name=name + "_grouped", tag=name + "_grouped", align_bytes=64)
+        def group_rows(name, raw, width, copy):
+            grouped = keep.tile([P, width * PACK], BF16, name=name + "_grouped", tag=name + "_grouped", align_bytes=64)
             copy(
                 grouped[:].rearrange("p (c i j) -> p c j i", i=4, j=PACK),
-                raw[:].rearrange("p j (c i) -> p c j i", i=4),
+                raw.rearrange("p j (c i) -> p c j i", i=4),
             )
-            return quantise(name, grouped[:], P)
+            return grouped
 
         def product(acc, stationary, moving):
             nc.tensor.matmul_mx(
                 out=acc,
-                lhsT=stationary[0][:].bitcast(FP8X4),
-                lhsT_scale=stationary[1][:],
+                lhsT=stationary[0].bitcast(FP8X4),
+                lhsT_scale=stationary[1],
                 rhs=moving[0].bitcast(FP8X4),
                 rhs_scale=moving[1],
                 start=True,
@@ -106,31 +102,33 @@ def tile_picked_hop2_gelu_p_kernel(tc, x_words, x_scales, w1, w2, gate, gate2, o
             return codes
 
         x_codes = [pick_words(0, "x_codes0")]
-        w1_q = [quantise_weight("w1_0", w1_raw[0], nc.scalar.copy)]
+        codes, scales = quantise("w1_0", group_rows("w1_0", w1_early[0][:], P, nc.scalar.copy)[:], P)
+        w1_q = [(codes[:], scales[:])]
         x_codes.append(pick_words(1, "w1_0_grouped"))
-        w1_q.append(quantise_weight("w1_1", w1_raw[1], nc.scalar.copy))
-        for t in range(2, TILES):
-            w1_q.append(quantise_weight(f"w1_{t}", w1_raw[t], nc.vector.tensor_copy))
+        second = group_rows("w1_1", w1_early[1][:], P, nc.scalar.copy)
+        rest = group_rows("w1_late", w1_late[:], 2 * P, nc.vector.tensor_copy)
+        codes, scales = quantise("w1_1", second[:], P)
+        w1_q.append((codes[:], scales[:]))
+        codes, scales = quantise("w1_late", rest[:], 2 * P)
+        w1_q.extend([(codes[:, :P], scales[:, :P]), (codes[:, P:], scales[:, P:])])
 
         h = [keep.tile([P, S], F32, name=f"h{t}") for t in range(TILES)]
 
         def hidden(t):
             weights = w1_q[t]
-            for c in range(halves):
-                cols = slice(c * BANK, (c + 1) * BANK)
-                acc = psum.tile([P, BANK], F32, name="h_acc")
-                product(acc[:], weights, (x_codes[c][:], x_bytes[:, cols]))
-                nc.scalar.activation(h[t][:, cols], acc[:], GELU)
+            pieces = ((0, 512), (512, 768), (768, 1024)) if t == 0 else ((0, 512), (512, 1024))
+            for j0, j1 in pieces:
+                c = j0 // BANK
+                acc = psum.tile([P, j1 - j0], F32, name="h_acc", bufs=3)
+                product(acc[:], weights, (x_codes[c][:, j0 - c * BANK : j1 - c * BANK], x_bytes[:, j0:j1]))
+                nc.scalar.activation(h[t][:, j0:j1], acc[:], GELU)
 
         z_rows = [keep.tile([P, (v1 - v0) // P, 2, P, 2], BF16, name=f"z_rows{v0}") for v0, v1 in GROUPS]
 
-        def aggregate(t, first, last):
+        def aggregate(t, first, last, terms):
             v0, v1 = GROUPS[first][0], GROUPS[last][1]
-            terms = []
             for d in range(2):
-                term = keep.tile([P, v1 - v0], F32, name=f"term{d}_{t}_{v0}")
-                nc.vector.tensor_tensor(term[:], h[t][:].indirect(pos[d][:, v0 // 16 : v1 // 16]), gates[d][:, v0:v1], MULT)
-                terms.append(term)
+                nc.vector.tensor_tensor(terms[d], h[t][:].indirect(pos[d][:, v0 // 16 : v1 // 16]), gates[d][:, v0:v1], MULT)
             turned = psum.tile([P, v1 - v0], F32, name="turned", tag="turned")
             for b in range((v1 - v0) // P):
                 cols = slice(b * P, (b + 1) * P)
@@ -149,7 +147,7 @@ def tile_picked_hop2_gelu_p_kernel(tc, x_words, x_scales, w1, w2, gate, gate2, o
             v0, v1 = GROUPS[g]
             blocks = (v1 - v0) // P
             words = z_rows[g][:].rearrange("v b u p e -> v (b u p e)").bitcast(F32)
-            back = psum.tile([P, blocks, 2, P], F32, name="back")
+            back = psum.tile([P, blocks, 2, P], F32, name="back", tag="back")
             for b in range(blocks):
                 for u in range(2):
                     nc.tensor.transpose(back[:, b, u, :], words[:, (2 * b + u) * P : (2 * b + u + 1) * P], ident[:])
@@ -163,23 +161,27 @@ def tile_picked_hop2_gelu_p_kernel(tc, x_words, x_scales, w1, w2, gate, gate2, o
         def second_layer(g, z_q, tag):
             v0, v1 = GROUPS[g]
             acc = psum.tile([P, v1 - v0], F32, name="g_acc", tag=tag)
-            product(acc[:], w2_q, (z_q[0][:], z_q[1][:]))
+            product(acc[:], (w2_q[0][:], w2_q[1][:]), (z_q[0][:], z_q[1][:]))
             nc.scalar.activation(g_all[:, v0:v1], acc[:], RELU)
 
         for t in range(TILES):
             hidden(t)
-        w2_q = quantise_weight("w2", w2_raw, nc.scalar.copy)
-        aggregate(0, 0, 2)
-        aggregate(1, 0, 2)
-        z_q = []
+        w2_grouped = group_rows("w2", w2_raw[:], N, nc.scalar.copy)
+        for t in range(2):
+            aggregate(t, 0, 2, [keep.tile([P, V], F32, name=f"term{t}_{d}")[:] for d in range(2)])
+        late = [[keep.tile([P, 2 * P], F32, name=f"late{k}_{d}", tag=f"late{k}_{d}", align_bytes=64) for d in range(2)] for k in range(2)]
+        aggregate(2, 0, 0, [late[0][d][:] for d in range(2)])
+        aggregate(3, 0, 0, [late[1][d][:] for d in range(2)])
+        aggregate(2, 1, 1, [late[0][d][:, :P] for d in range(2)])
+        z_q = [requantise(0)]
+        aggregate(3, 1, 1, [late[0][d][:, P:] for d in range(2)])
+        aggregate(2, 2, 2, [late[1][d][:, :P] for d in range(2)])
+        aggregate(3, 2, 2, [late[1][d][:, P:] for d in range(2)])
+        w2_q = quantise("w2", w2_grouped[:], N, "late1_1")
+        z_q.append(requantise(1))
+        z_q.append(requantise(2))
         for g in range(len(GROUPS)):
-            aggregate(2, g, g)
-            if g > 0:
-                z_q.append(requantise(g - 1))
-            aggregate(3, g, g)
-        z_q.append(requantise(len(GROUPS) - 1))
-        for g in range(len(GROUPS)):
-            second_layer(g, z_q[g], "turned" if g < len(GROUPS) - 1 else "g_acc")
+            second_layer(g, z_q[g], "turned" if g < len(GROUPS) - 1 else "back")
 
         roots = [keep.tile([P, U], F32, name=f"root{d}") for d in range(2)]
         for d in range(2):

@@ -20,66 +20,41 @@ RELU = mybir.ActivationFunctionType.Relu
 
 P = 128
 PACK = 4
+STRIPE = 16
 BANK = 512
+ALIGN = 64
 TILES = H // P
+SCALE_ROWS = K // 32
+SPREAD = P // SCALE_ROWS
 GROUPS = ((0, 256), (256, 384), (384, 512))
-WORDS_FIRST = 1024
+W1_REST_AT = 0
+W1_REST_BYTES = PACK * (H - P) * 4
+SCALE_TABLE_AT = W1_REST_BYTES - 1024
+W1_FIRST_GROUPED_AT = W1_REST_BYTES
+GATES_AT = W1_FIRST_GROUPED_AT + P * PACK * 2
 
 
 def tile_picked_hop2_gelu_p_kernel(tc, x_words, x_scales, w1, w2, gate, gate2, offs, pos1, pos2, nxt1, nxt2, out):
     nc = tc.nc
     with ExitStack() as ctx:
         keep = ctx.enter_context(tc.tile_pool(name="keep", bufs=1))
+        reused = ctx.enter_context(tc.tile_pool(name="reused", bufs=1))
         psum = ctx.enter_context(tc.psum_pool(name="psum", bufs=2))
 
         def load_list(name, src):
-            tile = keep.tile(list(src.shape), U16, name=name)
-            nc.sync.dma_start(tile[:], src)
-            return tile
+            offsets = keep.tile(list(src.shape), U16, name=name)
+            nc.sync.dma_start(offsets[:], src)
+            return offsets
 
-        ident = keep.tile([P, P], F32, name="ident")
-        make_identity(nc, ident[:])
-
-        scale_table = keep.tile([P, T], U8, name="scale_table")
-        nc.vector.memset(scale_table[:].bitcast(I32), 0)
-
-        word_table = keep.tile([P, T], U32, name="word_table")
-        words_hbm = x_words[0].rearrange("p n t -> p (n t)").bitcast(I32)
-        offs_sb = load_list("offs_sb", offs)
-        nc.sync.dma_start(word_table[:, :WORDS_FIRST].bitcast(I32), words_hbm[:, :WORDS_FIRST])
-        for r in range(4):
-            nc.sync.dma_start(scale_table[r:P:32, :].bitcast(I32), x_scales[0, r:16:4, :].bitcast(I32))
-        nc.sync.dma_start(word_table[:, WORDS_FIRST:].bitcast(I32), words_hbm[:, WORDS_FIRST:])
-
-        w1_hbm = w1.rearrange("(p j) c -> p j c", j=PACK)
-        w1_early = [keep.tile([P, PACK, P], F32, name=f"w1_raw{t}") for t in range(2)]
-        w1_late = keep.tile([P, PACK, 2 * P], F32, name="w1_late")
-        gates = [keep.tile([P, V], F32, name=f"gate{d}") for d in range(2)]
-        for t in range(2):
-            nc.sync.dma_start(w1_early[t][:], w1_hbm[:, :, t * P : (t + 1) * P])
-        nc.sync.dma_start(w1_late[:], w1_hbm[:, :, 2 * P :])
-        pos = [load_list("pos1_sb", pos1), load_list("pos2_sb", pos2)]
-        for d in range(2):
-            nc.sync.dma_start(gates[d][:], gate[d])
-        w2_raw = keep.tile([P, PACK, N], F32, name="w2_raw")
-        nc.sync.dma_start(w2_raw[:], w2.rearrange("(p j) c -> p j c", j=PACK))
-        nxt = [load_list("nxt1_sb", nxt1), load_list("nxt2_sb", nxt2)]
-        gates2 = keep.tile([P, 2, U], F32, name="gates2")
-        nc.sync.dma_start(gates2[:], gate2.rearrange("d p r -> p d r"))
-
-        def quantise(name, values, width, codes_tag=""):
-            codes = keep.tile([P, width], U32, name=name + "_codes", tag=codes_tag or name + "_codes", align_bytes=64)
-            scales = keep.tile([P, width], U8, name=name + "_scales", align_bytes=64)
-            nc.vector.quantize_mx(out=codes[:].bitcast(FP8X4), scales=scales[:], in_=values)
-            return codes, scales
-
-        def group_rows(name, raw, width, copy):
-            grouped = keep.tile([P, width * PACK], BF16, name=name + "_grouped", tag=name + "_grouped", align_bytes=64)
-            copy(
-                grouped[:].rearrange("p (c i j) -> p c j i", i=4, j=PACK),
-                raw.rearrange("p j (c i) -> p c j i", i=4),
-            )
+        def group_rows(grouped, raw, copy):
+            copy(grouped[:].rearrange("p (c j) -> p c j", j=PACK), raw.rearrange("p j c -> p c j"))
             return grouped
+
+        def quantise(name, grouped, width, codes_tag):
+            codes = keep.tile([P, width], U32, name=name + "_codes", tag=codes_tag, align_bytes=ALIGN)
+            scales = keep.tile([P, width], U8, name=name + "_scales", align_bytes=ALIGN)
+            nc.vector.quantize_mx(out=codes[:].bitcast(FP8X4), scales=scales[:], in_=grouped[:])
+            return codes, scales
 
         def product(acc, stationary, moving):
             nc.tensor.matmul_mx(
@@ -92,43 +67,72 @@ def tile_picked_hop2_gelu_p_kernel(tc, x_words, x_scales, w1, w2, gate, gate2, o
                 stop=True,
             )
 
-        x_bytes = keep.tile([P, S], U8, name="x_bytes", align_bytes=64)
-        nc.vector.tensor_copy(x_bytes[:], scale_table[:].indirect(offs_sb[:]))
-        halves = S // BANK
+        scale_table = reused.tile([P, T], U8, name="scale_table", offset=SCALE_TABLE_AT)
+        nc.gpsimd.memset(scale_table[:, : T // 2].bitcast(I32), 0)
+        nc.vector.memset(scale_table[:, T // 2 :].bitcast(I32), 0)
 
-        def pick_words(c, tag):
-            codes = keep.tile([P, BANK], U32, name=f"x_codes{c}", tag=tag, align_bytes=64)
-            nc.vector.tensor_copy(codes[:], word_table[:].indirect(offs_sb[:, c * BANK // 16 : (c + 1) * BANK // 16]))
-            return codes
+        ident = keep.tile([P, P], F32, name="ident")
+        make_identity(nc, ident[:])
 
-        x_codes = [pick_words(0, "x_codes0")]
-        codes, scales = quantise("w1_0", group_rows("w1_0", w1_early[0][:], P, nc.scalar.copy)[:], P)
+        word_table = keep.tile([P, T], U32, name="word_table", tag="word_table")
+        w1_hbm = w1.rearrange("(p j) c -> p j c", j=PACK)
+        w1_first = keep.tile([P, PACK, P], F32, name="w1_first")
+        offs_sb = load_list("offs_sb", offs)
+        nc.sync.dma_start(w1_first[:], w1_hbm[:, :, :P])
+        nc.sync.dma_start(scale_table[0:P:SPREAD, :].bitcast(I32), x_scales[0].bitcast(I32))
+        pos = [load_list("pos1_sb", pos1), load_list("pos2_sb", pos2)]
+        nxt = [load_list("nxt1_sb", nxt1), load_list("nxt2_sb", nxt2)]
+        nc.sync.dma_start(word_table[:].bitcast(I32), x_words[0].rearrange("p n t -> p (n t)").bitcast(I32))
+
+        picked_bytes = keep.tile([P, S], U8, name="picked_bytes")
+        nc.vector.tensor_copy(picked_bytes[:], scale_table[:].indirect(offs_sb[:]))
+        x_bytes = keep.tile([P, S], U8, name="x_bytes", align_bytes=ALIGN)
+        for r in range(4):
+            nc.sync.dma_start(x_bytes[r:P:32, :].bitcast(I32), picked_bytes[SPREAD * r : P : 32, :].bitcast(I32))
+        w1_rest = reused.tile([P, PACK, H - P], F32, name="w1_rest", offset=W1_REST_AT)
+        nc.sync.dma_start(w1_rest[:], w1_hbm[:, :, P:])
+        gates = reused.tile([P, 2, V], F32, name="gates", offset=GATES_AT)
+        nc.sync.dma_start(gates[:], gate.rearrange("d p v -> p d v"))
+
+        w1_first_grouped = reused.tile([P, P * PACK], BF16, name="w1_first_grouped", offset=W1_FIRST_GROUPED_AT, align_bytes=ALIGN)
+        codes, scales = quantise("w1_first", group_rows(w1_first_grouped, w1_first[:], nc.vector.tensor_copy), P, "w1_first_codes")
         w1_q = [(codes[:], scales[:])]
-        x_codes.append(pick_words(1, "w1_0_grouped"))
-        second = group_rows("w1_1", w1_early[1][:], P, nc.scalar.copy)
-        rest = group_rows("w1_late", w1_late[:], 2 * P, nc.vector.tensor_copy)
-        codes, scales = quantise("w1_1", second[:], P)
+
+        x_codes = [keep.tile([P, BANK], U32, name=f"x_codes{c}", align_bytes=ALIGN) for c in range(S // BANK)]
+        for c in range(S // BANK):
+            nc.vector.tensor_copy(x_codes[c][:], word_table[:].indirect(offs_sb[:, c * BANK // STRIPE : (c + 1) * BANK // STRIPE]))
+
+        w2_raw = keep.tile([P, PACK, N], F32, name="w2_raw", tag="word_table")
+        nc.sync.dma_start(w2_raw[:], w2.rearrange("(p j) c -> p j c", j=PACK))
+
+        w1_second_grouped = keep.tile([P, P * PACK], BF16, name="w1_second_grouped", align_bytes=ALIGN)
+        group_rows(w1_second_grouped, w1_rest[:, :, :P], nc.vector.tensor_copy)
+        w1_last_grouped = keep.tile([P, 2 * P * PACK], BF16, name="w1_last_grouped", align_bytes=ALIGN)
+        group_rows(w1_last_grouped, w1_rest[:, :, P:], nc.vector.tensor_copy)
+        gates2 = reused.tile([P, 2, U], F32, name="gates2", offset=W1_REST_AT)
+        nc.sync.dma_start(gates2[:], gate2.rearrange("d p r -> p d r"))
+        codes, scales = quantise("w1_second", w1_second_grouped, P, "w1_second_codes")
         w1_q.append((codes[:], scales[:]))
-        codes, scales = quantise("w1_late", rest[:], 2 * P)
+        codes, scales = quantise("w1_last", w1_last_grouped, 2 * P, "w1_last_codes")
         w1_q.extend([(codes[:, :P], scales[:, :P]), (codes[:, P:], scales[:, P:])])
 
         h = [keep.tile([P, S], F32, name=f"h{t}") for t in range(TILES)]
-
-        def hidden(t):
-            weights = w1_q[t]
-            pieces = ((0, 512), (512, 768), (768, 1024)) if t == 0 else ((0, 512), (512, 1024))
-            for j0, j1 in pieces:
-                c = j0 // BANK
-                acc = psum.tile([P, j1 - j0], F32, name="h_acc", bufs=3)
-                product(acc[:], weights, (x_codes[c][:, j0 - c * BANK : j1 - c * BANK], x_bytes[:, j0:j1]))
-                nc.scalar.activation(h[t][:, j0:j1], acc[:], GELU)
+        for t in range(TILES):
+            width = BANK // 2 if t == 0 else BANK
+            for j0 in range(0, S, width):
+                c, at = divmod(j0, BANK)
+                acc = psum.tile([P, width], F32, name="h_acc", bufs=4)
+                product(acc[:], w1_q[t], (x_codes[c][:, at : at + width], x_bytes[:, j0 : j0 + width]))
+                nc.scalar.activation(h[t][:, j0 : j0 + width], acc[:], GELU)
+        w2_grouped = keep.tile([P, N * PACK], BF16, name="w2_grouped", align_bytes=ALIGN)
+        group_rows(w2_grouped, w2_raw[:], nc.scalar.copy)
 
         z_rows = [keep.tile([P, (v1 - v0) // P, 2, P, 2], BF16, name=f"z_rows{v0}") for v0, v1 in GROUPS]
 
         def aggregate(t, first, last, terms):
             v0, v1 = GROUPS[first][0], GROUPS[last][1]
             for d in range(2):
-                nc.vector.tensor_tensor(terms[d], h[t][:].indirect(pos[d][:, v0 // 16 : v1 // 16]), gates[d][:, v0:v1], MULT)
+                nc.vector.tensor_tensor(terms[d], h[t][:].indirect(pos[d][:, v0 // STRIPE : v1 // STRIPE]), gates[:, d, v0:v1], MULT)
             turned = psum.tile([P, v1 - v0], F32, name="turned", tag="turned")
             for b in range((v1 - v0) // P):
                 cols = slice(b * P, (b + 1) * P)
@@ -138,38 +142,27 @@ def tile_picked_hop2_gelu_p_kernel(tc, x_words, x_scales, w1, w2, gate, gate2, o
                 g0, g1 = GROUPS[g]
                 nc.scalar.copy(
                     z_rows[g][:, :, :, 32 * t : 32 * (t + 1), :],
-                    turned[:, g0 - v0 : g1 - v0].rearrange("v (b p u e) -> v b u p e", p=32, u=2, e=2),
+                    turned[:, g0 - v0 : g1 - v0].rearrange("v (b m u e) -> v b u m e", m=32, u=2, e=2),
                 )
-
-        g_all = keep.tile([P, V], F32, name="g_all")
 
         def requantise(g):
             v0, v1 = GROUPS[g]
             blocks = (v1 - v0) // P
-            words = z_rows[g][:].rearrange("v b u p e -> v (b u p e)").bitcast(F32)
+            pairs = z_rows[g][:].rearrange("v b u p e -> v (b u p e)").bitcast(F32)
             back = psum.tile([P, blocks, 2, P], F32, name="back", tag="back")
             for b in range(blocks):
                 for u in range(2):
-                    nc.tensor.transpose(back[:, b, u, :], words[:, (2 * b + u) * P : (2 * b + u + 1) * P], ident[:])
-            z_grouped = keep.tile([P, (v1 - v0) * PACK], BF16, name=f"z_grouped{g}", align_bytes=64)
+                    nc.tensor.transpose(back[:, b, u, :], pairs[:, (2 * b + u) * P : (2 * b + u + 1) * P], ident[:])
+            z_grouped = keep.tile([P, (v1 - v0) * PACK], BF16, name=f"z_grouped{g}", align_bytes=ALIGN)
             nc.scalar.copy(
                 z_grouped[:].bitcast(F32).rearrange("p (b v u) -> p b v u", b=blocks, u=2),
                 back[:].rearrange("p b u v -> p b v u"),
             )
-            return quantise(f"z{g}", z_grouped[:], v1 - v0)
+            return quantise(f"z{g}", z_grouped, v1 - v0, f"z{g}_codes")
 
-        def second_layer(g, z_q, tag):
-            v0, v1 = GROUPS[g]
-            acc = psum.tile([P, v1 - v0], F32, name="g_acc", tag=tag)
-            product(acc[:], (w2_q[0][:], w2_q[1][:]), (z_q[0][:], z_q[1][:]))
-            nc.scalar.activation(g_all[:, v0:v1], acc[:], RELU)
-
-        for t in range(TILES):
-            hidden(t)
-        w2_grouped = group_rows("w2", w2_raw[:], N, nc.scalar.copy)
         for t in range(2):
             aggregate(t, 0, 2, [keep.tile([P, V], F32, name=f"term{t}_{d}")[:] for d in range(2)])
-        late = [[keep.tile([P, 2 * P], F32, name=f"late{k}_{d}", tag=f"late{k}_{d}", align_bytes=64) for d in range(2)] for k in range(2)]
+        late = [[keep.tile([P, 2 * P], F32, name=f"late{k}_{d}", tag=f"late{k}_{d}", align_bytes=ALIGN) for d in range(2)] for k in range(2)]
         aggregate(2, 0, 0, [late[0][d][:] for d in range(2)])
         aggregate(3, 0, 0, [late[1][d][:] for d in range(2)])
         aggregate(2, 1, 1, [late[0][d][:, :P] for d in range(2)])
@@ -177,11 +170,15 @@ def tile_picked_hop2_gelu_p_kernel(tc, x_words, x_scales, w1, w2, gate, gate2, o
         aggregate(3, 1, 1, [late[0][d][:, P:] for d in range(2)])
         aggregate(2, 2, 2, [late[1][d][:, :P] for d in range(2)])
         aggregate(3, 2, 2, [late[1][d][:, P:] for d in range(2)])
-        w2_q = quantise("w2", w2_grouped[:], N, "late1_1")
+        w2_q = quantise("w2", w2_grouped, N, "late1_1")
         z_q.append(requantise(1))
         z_q.append(requantise(2))
-        for g in range(len(GROUPS)):
-            second_layer(g, z_q[g], "turned" if g < len(GROUPS) - 1 else "back")
+
+        g_all = keep.tile([P, V], F32, name="g_all")
+        for g, (v0, v1) in enumerate(GROUPS):
+            acc = psum.tile([P, v1 - v0], F32, name="g_acc", tag="turned" if g < len(GROUPS) - 1 else "back")
+            product(acc[:], (w2_q[0][:], w2_q[1][:]), (z_q[g][0][:], z_q[g][1][:]))
+            nc.scalar.activation(g_all[:, v0:v1], acc[:], RELU)
 
         roots = [keep.tile([P, U], F32, name=f"root{d}") for d in range(2)]
         for d in range(2):

from contextlib import ExitStack

import concourse.mybir as mybir
from concourse.masks import make_identity

K, T, S, V, H, N, U = 512, 4096, 1024, 512, 512, 128, 256
FLOPS = 2 * K * H * S + 2 * H * N * V

F32 = mybir.dt.float32
BF16 = mybir.dt.bfloat16
I32 = mybir.dt.int32
U32 = mybir.dt.uint32
U16 = mybir.dt.uint16
U8 = mybir.dt.uint8
FP8X4 = mybir.dt.float8_e4m3fn_x4
MULT = mybir.AluOpType.mult
ADD = mybir.AluOpType.add
GELU = mybir.ActivationFunctionType.Gelu_apprx_tanh
RELU = mybir.ActivationFunctionType.Relu

P = 128
PACK = 4
STRIPE = 16
BANK = 512
ALIGN = 64
TILES = H // P
SCALE_ROWS = K // 32
SPREAD = P // SCALE_ROWS
GROUPS = ((0, 256), (256, 384), (384, 512))
W1_REST_AT = 0
W1_REST_BYTES = PACK * (H - P) * 4
SCALE_TABLE_AT = W1_REST_BYTES - 1024
W1_FIRST_GROUPED_AT = W1_REST_BYTES
GATES_AT = W1_FIRST_GROUPED_AT + P * PACK * 2


def tile_picked_hop2_gelu_p_kernel(tc, x_words, x_scales, w1, w2, gate, gate2, offs, pos1, pos2, nxt1, nxt2, out):
    nc = tc.nc
    with ExitStack() as ctx:
        keep = ctx.enter_context(tc.tile_pool(name="keep", bufs=1))
        reused = ctx.enter_context(tc.tile_pool(name="reused", bufs=1))
        psum = ctx.enter_context(tc.psum_pool(name="psum", bufs=2))

        def load_list(name, src):
            offsets = keep.tile(list(src.shape), U16, name=name)
            nc.sync.dma_start(offsets[:], src)
            return offsets

        def group_rows(grouped, raw, copy):
            copy(grouped[:].rearrange("p (c j) -> p c j", j=PACK), raw.rearrange("p j c -> p c j"))
            return grouped

        def quantise(name, grouped, width, codes_tag):
            codes = keep.tile([P, width], U32, name=name + "_codes", tag=codes_tag, align_bytes=ALIGN)
            scales = keep.tile([P, width], U8, name=name + "_scales", align_bytes=ALIGN)
            nc.vector.quantize_mx(out=codes[:].bitcast(FP8X4), scales=scales[:], in_=grouped[:])
            return codes, scales

        def product(acc, stationary, moving):
            nc.tensor.matmul_mx(
                out=acc,
                lhsT=stationary[0].bitcast(FP8X4),
                lhsT_scale=stationary[1],
                rhs=moving[0].bitcast(FP8X4),
                rhs_scale=moving[1],
                start=True,
                stop=True,
            )

        scale_table = reused.tile([P, T], U8, name="scale_table", offset=SCALE_TABLE_AT)
        nc.gpsimd.memset(scale_table[:, : T // 2].bitcast(I32), 0)
        nc.vector.memset(scale_table[:, T // 2 :].bitcast(I32), 0)

        ident = keep.tile([P, P], F32, name="ident")
        make_identity(nc, ident[:])

        word_table = keep.tile([P, T], U32, name="word_table", tag="word_table")
        w1_hbm = w1.rearrange("(p j) c -> p j c", j=PACK)
        w1_first = keep.tile([P, PACK, P], F32, name="w1_first")
        offs_sb = load_list("offs_sb", offs)
        nc.sync.dma_start(w1_first[:], w1_hbm[:, :, :P])
        nc.sync.dma_start(scale_table[0:P:SPREAD, :].bitcast(I32), x_scales[0].bitcast(I32))
        pos = [load_list("pos1_sb", pos1), load_list("pos2_sb", pos2)]
        nxt = [load_list("nxt1_sb", nxt1), load_list("nxt2_sb", nxt2)]
        nc.sync.dma_start(word_table[:].bitcast(I32), x_words[0].rearrange("p n t -> p (n t)").bitcast(I32))

        picked_bytes = keep.tile([P, S], U8, name="picked_bytes")
        nc.vector.tensor_copy(picked_bytes[:], scale_table[:].indirect(offs_sb[:]))
        x_bytes = keep.tile([P, S], U8, name="x_bytes", align_bytes=ALIGN)
        for r in range(4):
            nc.sync.dma_start(x_bytes[r:P:32, :].bitcast(I32), picked_bytes[SPREAD * r : P : 32, :].bitcast(I32))
        w1_rest = reused.tile([P, PACK, H - P], F32, name="w1_rest", offset=W1_REST_AT)
        nc.sync.dma_start(w1_rest[:], w1_hbm[:, :, P:])
        gates = reused.tile([P, 2, V], F32, name="gates", offset=GATES_AT)
        nc.sync.dma_start(gates[:], gate.rearrange("d p v -> p d v"))

        w1_first_grouped = reused.tile([P, P * PACK], BF16, name="w1_first_grouped", offset=W1_FIRST_GROUPED_AT, align_bytes=ALIGN)
        codes, scales = quantise("w1_first", group_rows(w1_first_grouped, w1_first[:], nc.vector.tensor_copy), P, "w1_first_codes")
        w1_q = [(codes[:], scales[:])]

        x_codes = [keep.tile([P, BANK], U32, name=f"x_codes{c}", align_bytes=ALIGN) for c in range(S // BANK)]
        for c in range(S // BANK):
            nc.vector.tensor_copy(x_codes[c][:], word_table[:].indirect(offs_sb[:, c * BANK // STRIPE : (c + 1) * BANK // STRIPE]))

        w2_raw = keep.tile([P, PACK, N], F32, name="w2_raw", tag="word_table")
        nc.sync.dma_start(w2_raw[:], w2.rearrange("(p j) c -> p j c", j=PACK))

        w1_second_grouped = keep.tile([P, P * PACK], BF16, name="w1_second_grouped", align_bytes=ALIGN)
        group_rows(w1_second_grouped, w1_rest[:, :, :P], nc.vector.tensor_copy)
        w1_last_grouped = keep.tile([P, 2 * P * PACK], BF16, name="w1_last_grouped", align_bytes=ALIGN)
        group_rows(w1_last_grouped, w1_rest[:, :, P:], nc.vector.tensor_copy)
        gates2 = reused.tile([P, 2, U], F32, name="gates2", offset=W1_REST_AT)
        nc.sync.dma_start(gates2[:], gate2.rearrange("d p r -> p d r"))
        codes, scales = quantise("w1_second", w1_second_grouped, P, "w1_second_codes")
        w1_q.append((codes[:], scales[:]))
        codes, scales = quantise("w1_last", w1_last_grouped, 2 * P, "w1_last_codes")
        w1_q.extend([(codes[:, :P], scales[:, :P]), (codes[:, P:], scales[:, P:])])

        h = [keep.tile([P, S], F32, name=f"h{t}") for t in range(TILES)]
        for t in range(TILES):
            width = BANK // 2 if t == 0 else BANK
            for j0 in range(0, S, width):
                c, at = divmod(j0, BANK)
                acc = psum.tile([P, width], F32, name="h_acc", bufs=4)
                product(acc[:], w1_q[t], (x_codes[c][:, at : at + width], x_bytes[:, j0 : j0 + width]))
                nc.scalar.activation(h[t][:, j0 : j0 + width], acc[:], GELU)
        w2_grouped = keep.tile([P, N * PACK], BF16, name="w2_grouped", align_bytes=ALIGN)
        group_rows(w2_grouped, w2_raw[:], nc.scalar.copy)

        z_rows = [keep.tile([P, (v1 - v0) // P, 2, P, 2], BF16, name=f"z_rows{v0}") for v0, v1 in GROUPS]

        def aggregate(t, first, last, terms):
            v0, v1 = GROUPS[first][0], GROUPS[last][1]
            for d in range(2):
                nc.vector.tensor_tensor(terms[d], h[t][:].indirect(pos[d][:, v0 // STRIPE : v1 // STRIPE]), gates[:, d, v0:v1], MULT)
            turned = psum.tile([P, v1 - v0], F32, name="turned", tag="turned")
            for b in range((v1 - v0) // P):
                cols = slice(b * P, (b + 1) * P)
                for d in range(2):
                    nc.tensor.matmul(turned[:, cols], terms[d][:, cols], ident[:], start=(d == 0), stop=(d == 1), is_transpose=True)
            for g in range(first, last + 1):
                g0, g1 = GROUPS[g]
                nc.scalar.copy(
                    z_rows[g][:, :, :, 32 * t : 32 * (t + 1), :],
                    turned[:, g0 - v0 : g1 - v0].rearrange("v (b m u e) -> v b u m e", m=32, u=2, e=2),
                )

        def requantise(g):
            v0, v1 = GROUPS[g]
            blocks = (v1 - v0) // P
            pairs = z_rows[g][:].rearrange("v b u p e -> v (b u p e)").bitcast(F32)
            back = psum.tile([P, blocks, 2, P], F32, name="back", tag="back")
            for b in range(blocks):
                for u in range(2):
                    nc.tensor.transpose(back[:, b, u, :], pairs[:, (2 * b + u) * P : (2 * b + u + 1) * P], ident[:])
            z_grouped = keep.tile([P, (v1 - v0) * PACK], BF16, name=f"z_grouped{g}", align_bytes=ALIGN)
            nc.scalar.copy(
                z_grouped[:].bitcast(F32).rearrange("p (b v u) -> p b v u", b=blocks, u=2),
                back[:].rearrange("p b u v -> p b v u"),
            )
            return quantise(f"z{g}", z_grouped, v1 - v0, f"z{g}_codes")

        for t in range(2):
            aggregate(t, 0, 2, [keep.tile([P, V], F32, name=f"term{t}_{d}")[:] for d in range(2)])
        late = [[keep.tile([P, 2 * P], F32, name=f"late{k}_{d}", tag=f"late{k}_{d}", align_bytes=ALIGN) for d in range(2)] for k in range(2)]
        aggregate(2, 0, 0, [late[0][d][:] for d in range(2)])
        aggregate(3, 0, 0, [late[1][d][:] for d in range(2)])
        aggregate(2, 1, 1, [late[0][d][:, :P] for d in range(2)])
        z_q = [requantise(0)]
        aggregate(3, 1, 1, [late[0][d][:, P:] for d in range(2)])
        aggregate(2, 2, 2, [late[1][d][:, :P] for d in range(2)])
        aggregate(3, 2, 2, [late[1][d][:, P:] for d in range(2)])
        w2_q = quantise("w2", w2_grouped, N, "late1_1")
        z_q.append(requantise(1))
        z_q.append(requantise(2))

        g_all = keep.tile([P, V], F32, name="g_all")
        for g, (v0, v1) in enumerate(GROUPS):
            acc = psum.tile([P, v1 - v0], F32, name="g_acc", tag="turned" if g < len(GROUPS) - 1 else "back")
            product(acc[:], (w2_q[0][:], w2_q[1][:]), (z_q[g][0][:], z_q[g][1][:]))
            nc.scalar.activation(g_all[:, v0:v1], acc[:], RELU)

        roots = [keep.tile([P, U], F32, name=f"root{d}") for d in range(2)]
        for d in range(2):
            nc.vector.tensor_tensor(roots[d][:], g_all[:].indirect(nxt[d][:]), gates2[:, d, :], MULT)
        result = keep.tile([P, U], F32, name="result")
        nc.vector.tensor_tensor(result[:], roots[0][:], roots[1][:], ADD)
        nc.sync.dma_start(out, result[:])
